import numpy as np
import ml_dtypes


def mxq(x, axis, fmt="e4m3"):
    dtype, down = {"e4m3": (ml_dtypes.float8_e4m3fn, 7), "e5m2": (ml_dtypes.float8_e5m2, 14)}[fmt]
    v = np.moveaxis(np.asarray(x, np.float32).astype(ml_dtypes.bfloat16).astype(np.float64), axis, -1)
    blocks = v.reshape(v.shape[:-1] + (-1, 32))
    amax = np.abs(blocks).max(-1, keepdims=True)
    byte = np.maximum(np.where(amax > 0, np.frexp(amax)[1] - 1 + 127, 0) - down, 1)
    scale = np.exp2(byte - 127.0)
    codes = (blocks / scale).astype(np.float32).astype(dtype).astype(np.float64)
    return np.moveaxis((codes * scale).reshape(v.shape), -1, axis)


WIDE = False


def mx_kscale(k):
    if not WIDE:
        return np.ones(k)
    levels = np.array([30, -30])
    if k % 512:
        return np.exp2(np.random.permutation(np.resize(levels, k // 32))).repeat(32)
    a = np.empty((k // 512, 16))
    for p in range(k // 512):
        a[p, :8] = np.random.permutation(np.resize(levels, 8))
        for g in range(8):
            far = levels[np.abs(levels - a[p, g]) >= 10]
            a[p, g + 8] = far[np.random.randint(len(far))]
    return np.exp2(a.ravel()).repeat(32)


def f64(x):
    return np.asarray(x).astype(np.float64)


def striped8(idx):
    return np.asarray(idx).reshape(8, -1, 16).transpose(0, 2, 1).reshape(128, -1).astype(np.uint16)


def unstriped8(offs):
    return offs.reshape(8, 16, -1).transpose(0, 2, 1).reshape(8, -1).astype(np.int64)


def pick8(x, idx, run):
    r = np.arange(len(x))
    return x[r[:, None], idx[r % (8 * run) // run]]


E2M1 = np.array([0.0, 0.5, 1.0, 1.5, 2.0, 3.0, 4.0, 6.0, -0.0, -0.5, -1.0, -1.5, -2.0, -3.0, -4.0, -6.0])


def pack_weight(w, fmt):
    k, n = w.shape
    w = f64(np.asarray(w, np.float32).astype(ml_dtypes.bfloat16)).reshape(k // 32, 32, n)
    amax = np.abs(w).max(1)
    if fmt in ("e4m3", "e5m2"):
        byte = np.frexp(amax)[1] - 1 + 127 - (7 if fmt == "e4m3" else 14)
    else:
        mant, ex = np.frexp(amax / 6.0)
        byte = np.where(mant > 0.5, ex, ex - 1) + 127
    byte = np.clip(np.where(amax > 0, byte, 1), 1, 254)
    scaled = (w * np.exp2(127.0 - byte)[:, None, :]).reshape(k, n).astype(np.float32)
    by_word = np.ascontiguousarray(scaled.reshape(k // 512, 128, 4, n).transpose(0, 1, 3, 2))
    if fmt in ("e4m3", "e5m2"):
        words = by_word.astype(ml_dtypes.float8_e4m3fn if fmt == "e4m3" else ml_dtypes.float8_e5m2).view(np.uint8)
    else:
        c = by_word.astype(ml_dtypes.float4_e2m1fn).view(np.uint8) & 0xF
        words = (c[..., 0::2] | (c[..., 1::2] << 4)).reshape(k // 512, 128, 2 * n)
    return np.ascontiguousarray(words), np.ascontiguousarray(byte.astype(np.uint8).reshape(k // 512, 16, n))


def unpack_weight(words, scales, fmt):
    g, _, n = scales.shape
    words = np.ascontiguousarray(words).reshape(g, 128, n, -1)
    if fmt in ("e4m3", "e5m2"):
        vals = words.view(ml_dtypes.float8_e4m3fn if fmt == "e4m3" else ml_dtypes.float8_e5m2).astype(np.float64)
    else:
        nib = np.empty((g, 128, n, 4), np.uint8)
        nib[..., 0::2] = words & 0xF
        nib[..., 1::2] = words >> 4
        vals = E2M1[nib]
    vals = vals * np.repeat(np.exp2(scales.astype(np.float64) - 127.0), 8, axis=1)[..., None]
    return vals.transpose(0, 1, 3, 2).reshape(g * 512, n)


K, J, N, T = 256, 1024, 256, 2048


def setup_inputs():
    n = np.random.standard_normal
    idx = np.stack([np.random.permutation(T)[:J] for _ in range(8)])
    fj = mx_kscale(J)
    gjp = pack_weight(n((J, N)) * np.exp(0.5 * n((J, 1))) / fj[:, None], "e5m2")
    return {
        "xf": (n((K, T))).astype(np.float32),
        "ra": (np.random.uniform(0.5, 1.5, (1, J)) * fj).astype(np.float32),
        "gj_words": gjp[0],
        "gj_scales": gjp[1],
        "old": (1.0 * n((K, N))).astype(np.float32),
        "offs": striped8(idx),
    }


def reference(xf, ra, gj_words, gj_scales, old, offs):
    idx = unstriped8(offs)
    gju = unpack_weight(gj_words, gj_scales, "e5m2")
    us = pick8(f64(xf), idx, 16) * f64(ra)
    uj = us.T
    ujq = mxq(uj, 0, "e4m3")
    w = ujq.T @ gju
    pk1 = np.max(np.abs(w), axis=1, keepdims=True)
    y = w / (pk1 + 2.0) - 0.3 * f64(old)
    return y

@@ -1,0 +1,127 @@
+from contextlib import ExitStack
+
+import concourse.mybir as mybir
+from concourse.masks import make_identity
+
+K, J, N, T = 256, 1024, 256, 2048
+FLOPS = 2 * K * J * N
+
+F32 = mybir.dt.float32
+BF16 = mybir.dt.bfloat16
+I32 = mybir.dt.int32
+U32 = mybir.dt.uint32
+U16 = mybir.dt.uint16
+U8 = mybir.dt.uint8
+E4M3X4 = mybir.dt.float8_e4m3fn_x4
+E5M2X4 = mybir.dt.float8_e5m2_x4
+ALU = mybir.AluOpType
+ACT = mybir.ActivationFunctionType
+
+P = 128
+PACK = 4
+J_PASS = P * PACK
+PASSES = J // J_PASS
+K_TILES = K // P
+LIST_COLS = J_PASS // 16
+
+
+def tile_list_moment_headpicks_stored_rowpeaks_kernel(tc, xf, ra, gj_words, gj_scales, old, offs, out):
+    nc = tc.nc
+    with ExitStack() as ctx:
+        sb = ctx.enter_context(tc.tile_pool(name="sb", bufs=1))
+        ps = ctx.enter_context(tc.psum_pool(name="ps", bufs=1))
+
+        offsets = sb.tile([P, J // 16], U16, name="offsets")
+        nc.sync.dma_start(offsets[:], offs)
+        ra_cols = sb.tile([P, PASSES, PACK], F32, name="ra_cols")
+        nc.scalar.dma_start(ra_cols[:], ra.rearrange("o (z q t) -> q (o z) t", z=PASSES, t=PACK))
+        windows = [sb.tile([P, T], F32, name=f"window{c}") for c in range(K_TILES)]
+        for c in range(K_TILES):
+            nc.sync.dma_start(windows[c][:], xf[c * P : (c + 1) * P, :])
+        g_codes = sb.tile([P, PASSES, N], U32, name="g_codes", align_bytes=64)
+        nc.sync.dma_start(g_codes[:].bitcast(I32), gj_words.rearrange("z l c r -> l z (c r)").bitcast(I32))
+        g_scales = sb.tile([P, PASSES, N], U8, name="g_scales", align_bytes=64)
+        nc.vector.memset(g_scales[:].bitcast(I32), 0)
+        for quad in range(4):
+            nc.scalar.dma_start(
+                g_scales[32 * quad : 32 * quad + 4, :, :].bitcast(I32),
+                gj_scales[:, 4 * quad : 4 * quad + 4, :].rearrange("z r c -> r z c").bitcast(I32),
+            )
+        old_sb = sb.tile([P, K_TILES, N], F32, name="old_sb")
+        nc.sync.dma_start(old_sb[:], old.rearrange("(c p) n -> p c n", p=P))
+
+        ident = sb.tile([P, P], F32, name="ident")
+        make_identity(nc, ident[:])
+
+        ra_ps = [ps.tile([P, PACK, P], F32, name=f"ra_ps{z}") for z in range(PASSES)]
+        for z in range(PASSES):
+            for t in range(PACK):
+                nc.tensor.transpose(ra_ps[z][:, t, :], ra_cols[:, z, t : t + 1].to_broadcast([P, P]), ident[:])
+        ra_first = sb.tile([P, J_PASS], F32, name="ra_first")
+        nc.vector.tensor_copy(ra_first[:].rearrange("p (q t) -> p q t", t=PACK), ra_ps[0][:].rearrange("p t q -> p q t"))
+
+        def pick_and_turn(c):
+            weighted = sb.tile([P, J_PASS], F32, name=f"weighted{c}")
+            nc.vector.tensor_tensor(weighted[:], windows[c][:].indirect(offsets[:, 0:LIST_COLS]), ra_first[:], ALU.mult)
+            picked = sb.tile([P, J_PASS], F32, name=f"picked{c}")
+            nc.scalar.activation(picked[:], windows[c][:].indirect(offsets[:, LIST_COLS : 2 * LIST_COLS]), ACT.Copy)
+            pairs = [sb.tile([P, 2, P, 2], BF16, name=f"pairs{c}_{z}") for z in range(PASSES)]
+            nc.scalar.copy(pairs[0][:], weighted[:].rearrange("p (q u e) -> p u q e", u=2, e=2))
+            nc.vector.tensor_tensor(
+                pairs[1][:],
+                picked[:].rearrange("p (q u e) -> p u q e", u=2, e=2),
+                ra_ps[1][:].rearrange("p (u e) q -> p u q e", e=2),
+                ALU.mult,
+            )
+            grouped = []
+            for z in range(PASSES):
+                turned = ps.tile([P, 2, P], F32, name=f"turned{c}_{z}")
+                words = pairs[z][:].rearrange("p u q e -> p (u q e)").bitcast(F32)
+                for u in range(2):
+                    nc.tensor.transpose(turned[:, u, :], words[:, u * P : (u + 1) * P], ident[:])
+                rows = sb.tile([P, P * PACK], BF16, name=f"grouped{c}_{z}", align_bytes=64)
+                dst = rows[:].bitcast(F32).rearrange("p (k u) -> p k u", u=2)
+                src = turned[:].rearrange("p u k -> p k u")
+                if z == 0:
+                    nc.scalar.copy(dst, src)
+                else:
+                    nc.vector.tensor_copy(dst, src)
+                grouped.append(rows)
+            return grouped
+
+        def multiply(c, grouped):
+            acc = ps.tile([P, N], F32, name=f"acc{c}")
+            codes = [sb.tile([P, P], U32, name=f"codes{c}_{z}", align_bytes=64) for z in range(PASSES)]
+            scales = [sb.tile([P, P], U8, name=f"scales{c}_{z}", align_bytes=64) for z in range(PASSES)]
+            for z in range(PASSES):
+                nc.vector.quantize_mx(out=codes[z][:].bitcast(E4M3X4), scales=scales[z][:], in_=grouped[z][:])
+            for z in range(PASSES):
+                nc.tensor.matmul_mx(
+                    out=acc[:],
+                    lhsT=codes[z][:].bitcast(E4M3X4),
+                    lhsT_scale=scales[z][:],
+                    rhs=g_codes[:, z, :].bitcast(E5M2X4),
+                    rhs_scale=g_scales[:, z, :],
+                    start=(z == 0),
+                    stop=(z == PASSES - 1),
+                )
+            return acc
+
+        def finish(c, acc):
+            old_part = sb.tile([P, N], F32, name=f"old_part{c}")
+            nc.scalar.activation(old_part[:], old_sb[:, c, :], ACT.Copy, scale=0.3)
+            size = sb.tile([P, N], F32, name=f"size{c}")
+            nc.scalar.activation(size[:], acc[:], ACT.Abs)
+            raised = sb.tile([P, N], F32, name=f"raised{c}")
+            divisor = sb.tile([P, 1], F32, name=f"divisor{c}")
+            nc.vector.tensor_scalar(raised[:], size[:], 2.0, None, ALU.add, ALU.max, accum_out=divisor[:])
+            inverse = sb.tile([P, 1], F32, name=f"inverse{c}")
+            nc.vector.reciprocal(inverse[:], divisor[:])
+            result = sb.tile([P, N], F32, name=f"result{c}")
+            nc.vector.scalar_tensor_tensor(result[:], acc[:], inverse[:], old_part[:], ALU.mult, ALU.subtract)
+            nc.sync.dma_start(out[c * P : (c + 1) * P, :], result[:])
+
+        turned_tiles = [pick_and_turn(c) for c in range(K_TILES)]
+        sums = [multiply(c, turned_tiles[c]) for c in range(K_TILES)]
+        for c in range(K_TILES):
+            finish(c, sums[c])

@@ -29,21 +29,28 @@ def tile_list_moment_headpicks_stored_rowpeaks_kernel(tc, xf, ra, gj_words, gj_s
     nc = tc.nc
     with ExitStack() as ctx:
         sb = ctx.enter_context(tc.tile_pool(name="sb", bufs=1))
+        shared = ctx.enter_context(tc.tile_pool(name="shared", bufs=1))
         ps = ctx.enter_context(tc.psum_pool(name="ps", bufs=1))
 
+        warm_in = sb.tile([P, 1], F32, name="warm_in")
+        nc.vector.memset(warm_in[:], 0.0)
+        unread = sb.tile([P, 1], F32, name="unread")
+        nc.scalar.activation(unread[:], warm_in[:], ACT.Abs)
+
         offsets = sb.tile([P, J // 16], U16, name="offsets")
-        nc.sync.dma_start(offsets[:], offs)
         ra_cols = sb.tile([P, PASSES, PACK], F32, name="ra_cols")
-        nc.scalar.dma_start(ra_cols[:], ra.rearrange("o (z q t) -> q (o z) t", z=PASSES, t=PACK))
-        windows = [sb.tile([P, T], F32, name=f"window{c}") for c in range(K_TILES)]
+        nc.sync.dma_start(ra_cols[:], ra.rearrange("o (z q t) -> q (o z) t", z=PASSES, t=PACK))
+        windows = [shared.tile([P, T], F32, name="window0", offset=0), sb.tile([P, T], F32, name="window1")]
         for c in range(K_TILES):
             nc.sync.dma_start(windows[c][:], xf[c * P : (c + 1) * P, :])
+            if c == 0:
+                nc.sync.dma_start(offsets[:], offs)
         g_codes = sb.tile([P, PASSES, N], U32, name="g_codes", align_bytes=64)
         nc.sync.dma_start(g_codes[:].bitcast(I32), gj_words.rearrange("z l c r -> l z (c r)").bitcast(I32))
         g_scales = sb.tile([P, PASSES, N], U8, name="g_scales", align_bytes=64)
         nc.vector.memset(g_scales[:].bitcast(I32), 0)
         for quad in range(4):
-            nc.scalar.dma_start(
+            nc.sync.dma_start(
                 g_scales[32 * quad : 32 * quad + 4, :, :].bitcast(I32),
                 gj_scales[:, 4 * quad : 4 * quad + 4, :].rearrange("z r c -> r z c").bitcast(I32),
             )
@@ -53,32 +60,48 @@ def tile_list_moment_headpicks_stored_rowpeaks_kernel(tc, xf, ra, gj_words, gj_s
         ident = sb.tile([P, P], F32, name="ident")
         make_identity(nc, ident[:])
 
-        ra_ps = [ps.tile([P, PACK, P], F32, name=f"ra_ps{z}") for z in range(PASSES)]
-        for z in range(PASSES):
+        def spread_ra(z):
+            spread = ps.tile([P, PACK, P], F32, name=f"ra_spread{z}")
             for t in range(PACK):
-                nc.tensor.transpose(ra_ps[z][:, t, :], ra_cols[:, z, t : t + 1].to_broadcast([P, P]), ident[:])
+                nc.tensor.transpose(spread[:, t, :], ra_cols[:, z, t : t + 1].to_broadcast([P, P]), ident[:])
+            return spread
+
         ra_first = sb.tile([P, J_PASS], F32, name="ra_first")
-        nc.vector.tensor_copy(ra_first[:].rearrange("p (q t) -> p q t", t=PACK), ra_ps[0][:].rearrange("p t q -> p q t"))
+        nc.vector.tensor_copy(ra_first[:].rearrange("p (q t) -> p q t", t=PACK), spread_ra(0)[:].rearrange("p t q -> p q t"))
+        ra_second = spread_ra(1)
+
+        def place(shape, dtype, name, offset):
+            if offset is None:
+                return sb.tile(shape, dtype, name=name)
+            return shared.tile(shape, dtype, name=name, offset=offset)
 
         def pick_and_turn(c):
-            weighted = sb.tile([P, J_PASS], F32, name=f"weighted{c}")
+            weighted = place([P, J_PASS], F32, f"weighted{c}", 0 if c == 1 else None)
             nc.vector.tensor_tensor(weighted[:], windows[c][:].indirect(offsets[:, 0:LIST_COLS]), ra_first[:], ALU.mult)
-            picked = sb.tile([P, J_PASS], F32, name=f"picked{c}")
+            picked = place([P, J_PASS], F32, f"picked{c}", 2048 if c == 1 else None)
             nc.scalar.activation(picked[:], windows[c][:].indirect(offsets[:, LIST_COLS : 2 * LIST_COLS]), ACT.Copy)
-            pairs = [sb.tile([P, 2, P, 2], BF16, name=f"pairs{c}_{z}") for z in range(PASSES)]
-            nc.scalar.copy(pairs[0][:], weighted[:].rearrange("p (q u e) -> p u q e", u=2, e=2))
-            nc.vector.tensor_tensor(
-                pairs[1][:],
-                picked[:].rearrange("p (q u e) -> p u q e", u=2, e=2),
-                ra_ps[1][:].rearrange("p (u e) q -> p u q e", e=2),
-                ALU.mult,
-            )
+            pairs = [
+                [place([P, 2 * P], BF16, f"pairs{c}_{z}_{u}", 4096 + 1024 * z + 512 * ((u + c) % 2)) for u in range(2)]
+                for z in range(PASSES)
+            ]
+            turned_all = [ps.tile([P, 2, P], F32, name=f"turned{c}_{z}") for z in range(PASSES)]
+            for u in range(2):
+                nc.scalar.copy(
+                    pairs[0][u][:].rearrange("p (q e) -> p q e", e=2),
+                    weighted[:].rearrange("p (q u e) -> p u q e", u=2, e=2)[:, u],
+                )
+                nc.vector.tensor_tensor(
+                    pairs[1][u][:].rearrange("p (q e) -> p q e", e=2),
+                    picked[:].rearrange("p (q u e) -> p u q e", u=2, e=2)[:, u],
+                    ra_second[:].rearrange("p (u e) q -> p u q e", e=2)[:, u],
+                    ALU.mult,
+                )
+            for u in range(2):
+                for z in range(PASSES):
+                    nc.tensor.transpose(turned_all[z][:, u, :], pairs[z][u][:].bitcast(F32), ident[:])
             grouped = []
             for z in range(PASSES):
-                turned = ps.tile([P, 2, P], F32, name=f"turned{c}_{z}")
-                words = pairs[z][:].rearrange("p u q e -> p (u q e)").bitcast(F32)
-                for u in range(2):
-                    nc.tensor.transpose(turned[:, u, :], words[:, u * P : (u + 1) * P], ident[:])
+                turned = turned_all[z]
                 rows = sb.tile([P, P * PACK], BF16, name=f"grouped{c}_{z}", align_bytes=64)
                 dst = rows[:].bitcast(F32).rearrange("p (k u) -> p k u", u=2)
                 src = turned[:].rearrange("p u k -> p k u")
@@ -107,21 +130,24 @@ def tile_list_moment_headpicks_stored_rowpeaks_kernel(tc, xf, ra, gj_words, gj_s
                 )
             return acc
 
-        def finish(c, acc):
-            old_part = sb.tile([P, N], F32, name=f"old_part{c}")
-            nc.scalar.activation(old_part[:], old_sb[:, c, :], ACT.Copy, scale=0.3)
-            size = sb.tile([P, N], F32, name=f"size{c}")
+        def row_inverse(c, acc):
+            size = place([P, N], F32, f"size{c}", 6144 if c == 1 else None)
             nc.scalar.activation(size[:], acc[:], ACT.Abs)
-            raised = sb.tile([P, N], F32, name=f"raised{c}")
             divisor = sb.tile([P, 1], F32, name=f"divisor{c}")
-            nc.vector.tensor_scalar(raised[:], size[:], 2.0, None, ALU.add, ALU.max, accum_out=divisor[:])
+            nc.vector.tensor_scalar(size[:], size[:], 2.0, None, ALU.add, ALU.max, accum_out=divisor[:])
             inverse = sb.tile([P, 1], F32, name=f"inverse{c}")
             nc.vector.reciprocal(inverse[:], divisor[:])
-            result = sb.tile([P, N], F32, name=f"result{c}")
-            nc.vector.scalar_tensor_tensor(result[:], acc[:], inverse[:], old_part[:], ALU.mult, ALU.subtract)
+            return inverse
+
+        def finish(c, acc, inverse):
+            result = place([P, N], F32, f"result{c}", 6144 if c == 0 else None)
+            nc.vector.scalar_tensor_tensor(result[:], acc[:], inverse[:], old_part[:, c, :], ALU.mult, ALU.subtract)
             nc.sync.dma_start(out[c * P : (c + 1) * P, :], result[:])
 
         turned_tiles = [pick_and_turn(c) for c in range(K_TILES)]
+        old_part = place([P, K_TILES, N], F32, "old_part", 4096)
+        nc.scalar.activation(old_part[:], old_sb[:], ACT.Copy, scale=0.3)
         sums = [multiply(c, turned_tiles[c]) for c in range(K_TILES)]
+        inverses = [row_inverse(c, sums[c]) for c in range(K_TILES)]
         for c in range(K_TILES):
-            finish(c, sums[c])
+            finish(c, sums[c], inverses[c])

from contextlib import ExitStack

import concourse.mybir as mybir
from concourse.masks import make_identity

K, J, N, T = 256, 1024, 256, 2048
FLOPS = 2 * K * J * N

F32 = mybir.dt.float32
BF16 = mybir.dt.bfloat16
I32 = mybir.dt.int32
U32 = mybir.dt.uint32
U16 = mybir.dt.uint16
U8 = mybir.dt.uint8
E4M3X4 = mybir.dt.float8_e4m3fn_x4
E5M2X4 = mybir.dt.float8_e5m2_x4
ALU = mybir.AluOpType
ACT = mybir.ActivationFunctionType

P = 128
PACK = 4
J_PASS = P * PACK
PASSES = J // J_PASS
K_TILES = K // P
LIST_COLS = J_PASS // 16


def tile_list_moment_headpicks_stored_rowpeaks_kernel(tc, xf, ra, gj_words, gj_scales, old, offs, out):
    nc = tc.nc
    with ExitStack() as ctx:
        sb = ctx.enter_context(tc.tile_pool(name="sb", bufs=1))
        shared = ctx.enter_context(tc.tile_pool(name="shared", bufs=1))
        ps = ctx.enter_context(tc.psum_pool(name="ps", bufs=1))

        warm_in = sb.tile([P, 1], F32, name="warm_in")
        nc.vector.memset(warm_in[:], 0.0)
        unread = sb.tile([P, 1], F32, name="unread")
        nc.scalar.activation(unread[:], warm_in[:], ACT.Abs)

        offsets = sb.tile([P, J // 16], U16, name="offsets")
        ra_cols = sb.tile([P, PASSES, PACK], F32, name="ra_cols")
        nc.sync.dma_start(ra_cols[:], ra.rearrange("o (z q t) -> q (o z) t", z=PASSES, t=PACK))
        windows = [shared.tile([P, T], F32, name="window0", offset=0), sb.tile([P, T], F32, name="window1")]
        for c in range(K_TILES):
            nc.sync.dma_start(windows[c][:], xf[c * P : (c + 1) * P, :])
            if c == 0:
                nc.sync.dma_start(offsets[:], offs)
        g_codes = sb.tile([P, PASSES, N], U32, name="g_codes", align_bytes=64)
        nc.sync.dma_start(g_codes[:].bitcast(I32), gj_words.rearrange("z l c r -> l z (c r)").bitcast(I32))
        g_scales = sb.tile([P, PASSES, N], U8, name="g_scales", align_bytes=64)
        nc.vector.memset(g_scales[:].bitcast(I32), 0)
        for quad in range(4):
            nc.sync.dma_start(
                g_scales[32 * quad : 32 * quad + 4, :, :].bitcast(I32),
                gj_scales[:, 4 * quad : 4 * quad + 4, :].rearrange("z r c -> r z c").bitcast(I32),
            )
        old_sb = sb.tile([P, K_TILES, N], F32, name="old_sb")
        nc.sync.dma_start(old_sb[:], old.rearrange("(c p) n -> p c n", p=P))

        ident = sb.tile([P, P], F32, name="ident")
        make_identity(nc, ident[:])

        def spread_ra(z):
            spread = ps.tile([P, PACK, P], F32, name=f"ra_spread{z}")
            for t in range(PACK):
                nc.tensor.transpose(spread[:, t, :], ra_cols[:, z, t : t + 1].to_broadcast([P, P]), ident[:])
            return spread

        ra_first = sb.tile([P, J_PASS], F32, name="ra_first")
        nc.vector.tensor_copy(ra_first[:].rearrange("p (q t) -> p q t", t=PACK), spread_ra(0)[:].rearrange("p t q -> p q t"))
        ra_second = spread_ra(1)

        def place(shape, dtype, name, offset):
            if offset is None:
                return sb.tile(shape, dtype, name=name)
            return shared.tile(shape, dtype, name=name, offset=offset)

        def pick_and_turn(c):
            weighted = place([P, J_PASS], F32, f"weighted{c}", 0 if c == 1 else None)
            nc.vector.tensor_tensor(weighted[:], windows[c][:].indirect(offsets[:, 0:LIST_COLS]), ra_first[:], ALU.mult)
            picked = place([P, J_PASS], F32, f"picked{c}", 2048 if c == 1 else None)
            nc.scalar.activation(picked[:], windows[c][:].indirect(offsets[:, LIST_COLS : 2 * LIST_COLS]), ACT.Copy)
            pairs = [
                [place([P, 2 * P], BF16, f"pairs{c}_{z}_{u}", 4096 + 1024 * z + 512 * ((u + c) % 2)) for u in range(2)]
                for z in range(PASSES)
            ]
            turned_all = [ps.tile([P, 2, P], F32, name=f"turned{c}_{z}") for z in range(PASSES)]
            for u in range(2):
                nc.scalar.copy(
                    pairs[0][u][:].rearrange("p (q e) -> p q e", e=2),
                    weighted[:].rearrange("p (q u e) -> p u q e", u=2, e=2)[:, u],
                )
                nc.vector.tensor_tensor(
                    pairs[1][u][:].rearrange("p (q e) -> p q e", e=2),
                    picked[:].rearrange("p (q u e) -> p u q e", u=2, e=2)[:, u],
                    ra_second[:].rearrange("p (u e) q -> p u q e", e=2)[:, u],
                    ALU.mult,
                )
            for u in range(2):
                for z in range(PASSES):
                    nc.tensor.transpose(turned_all[z][:, u, :], pairs[z][u][:].bitcast(F32), ident[:])
            grouped = []
            for z in range(PASSES):
                turned = turned_all[z]
                rows = sb.tile([P, P * PACK], BF16, name=f"grouped{c}_{z}", align_bytes=64)
                dst = rows[:].bitcast(F32).rearrange("p (k u) -> p k u", u=2)
                src = turned[:].rearrange("p u k -> p k u")
                if z == 0:
                    nc.scalar.copy(dst, src)
                else:
                    nc.vector.tensor_copy(dst, src)
                grouped.append(rows)
            return grouped

        def multiply(c, grouped):
            acc = ps.tile([P, N], F32, name=f"acc{c}")
            codes = [sb.tile([P, P], U32, name=f"codes{c}_{z}", align_bytes=64) for z in range(PASSES)]
            scales = [sb.tile([P, P], U8, name=f"scales{c}_{z}", align_bytes=64) for z in range(PASSES)]
            for z in range(PASSES):
                nc.vector.quantize_mx(out=codes[z][:].bitcast(E4M3X4), scales=scales[z][:], in_=grouped[z][:])
            for z in range(PASSES):
                nc.tensor.matmul_mx(
                    out=acc[:],
                    lhsT=codes[z][:].bitcast(E4M3X4),
                    lhsT_scale=scales[z][:],
                    rhs=g_codes[:, z, :].bitcast(E5M2X4),
                    rhs_scale=g_scales[:, z, :],
                    start=(z == 0),
                    stop=(z == PASSES - 1),
                )
            return acc

        def row_inverse(c, acc):
            size = place([P, N], F32, f"size{c}", 6144 if c == 1 else None)
            nc.scalar.activation(size[:], acc[:], ACT.Abs)
            divisor = sb.tile([P, 1], F32, name=f"divisor{c}")
            nc.vector.tensor_scalar(size[:], size[:], 2.0, None, ALU.add, ALU.max, accum_out=divisor[:])
            inverse = sb.tile([P, 1], F32, name=f"inverse{c}")
            nc.vector.reciprocal(inverse[:], divisor[:])
            return inverse

        def finish(c, acc, inverse):
            result = place([P, N], F32, f"result{c}", 6144 if c == 0 else None)
            nc.vector.scalar_tensor_tensor(result[:], acc[:], inverse[:], old_part[:, c, :], ALU.mult, ALU.subtract)
            nc.sync.dma_start(out[c * P : (c + 1) * P, :], result[:])

        turned_tiles = [pick_and_turn(c) for c in range(K_TILES)]
        old_part = place([P, K_TILES, N], F32, "old_part", 4096)
        nc.scalar.activation(old_part[:], old_sb[:], ACT.Copy, scale=0.3)
        sums = [multiply(c, turned_tiles[c]) for c in range(K_TILES)]
        inverses = [row_inverse(c, sums[c]) for c in range(K_TILES)]
        for c in range(K_TILES):
            finish(c, sums[c], inverses[c])
